import numpy as np
import ml_dtypes


def mxq(x, axis, fmt="e4m3"):
    dtype, down = {"e4m3": (ml_dtypes.float8_e4m3fn, 7), "e5m2": (ml_dtypes.float8_e5m2, 14)}[fmt]
    v = np.moveaxis(np.asarray(x, np.float32).astype(ml_dtypes.bfloat16).astype(np.float64), axis, -1)
    blocks = v.reshape(v.shape[:-1] + (-1, 32))
    amax = np.abs(blocks).max(-1, keepdims=True)
    byte = np.maximum(np.where(amax > 0, np.frexp(amax)[1] - 1 + 127, 0) - down, 1)
    scale = np.exp2(byte - 127.0)
    codes = (blocks / scale).astype(np.float32).astype(dtype).astype(np.float64)
    return np.moveaxis((codes * scale).reshape(v.shape), -1, axis)


WIDE = False


def mx_kscale(k):
    if not WIDE:
        return np.ones(k)
    levels = np.array([10, -10, 5, -5, 0])
    if k % 512:
        return np.exp2(np.random.permutation(np.resize(levels, k // 32))).repeat(32)
    a = np.empty((k // 512, 16))
    for p in range(k // 512):
        a[p, :8] = np.random.permutation(np.resize(levels, 8))
        for g in range(8):
            far = levels[np.abs(levels - a[p, g]) >= 10]
            a[p, g + 8] = far[np.random.randint(len(far))]
    return np.exp2(a.ravel()).repeat(32)


def f64(x):
    return np.asarray(x).astype(np.float64)


def striped(idx):
    return np.tile(idx.reshape(-1, 16).T, (8, 1)).astype(np.uint16)


def unstriped(offs):
    return offs[:16].T.reshape(-1).astype(np.int64)


E2M1 = np.array([0.0, 0.5, 1.0, 1.5, 2.0, 3.0, 4.0, 6.0, -0.0, -0.5, -1.0, -1.5, -2.0, -3.0, -4.0, -6.0])


def pack_weight(w, fmt):
    k, n = w.shape
    w = f64(np.asarray(w, np.float32).astype(ml_dtypes.bfloat16)).reshape(k // 32, 32, n)
    amax = np.abs(w).max(1)
    if fmt == "e4m3":
        byte = np.frexp(amax)[1] - 1 + 127 - 7
    else:
        mant, ex = np.frexp(amax / 6.0)
        byte = np.where(mant > 0.5, ex, ex - 1) + 127
    byte = np.clip(np.where(amax > 0, byte, 1), 1, 254)
    scaled = (w * np.exp2(127.0 - byte)[:, None, :]).reshape(k, n).astype(np.float32)
    by_word = np.ascontiguousarray(scaled.reshape(k // 512, 128, 4, n).transpose(0, 1, 3, 2))
    if fmt == "e4m3":
        words = by_word.astype(ml_dtypes.float8_e4m3fn).view(np.uint8)
    else:
        c = by_word.astype(ml_dtypes.float4_e2m1fn).view(np.uint8) & 0xF
        words = (c[..., 0::2] | (c[..., 1::2] << 4)).reshape(k // 512, 128, 2 * n)
    return np.ascontiguousarray(words), np.ascontiguousarray(byte.astype(np.uint8).reshape(k // 512, 16, n))


def unpack_weight(words, scales, fmt):
    g, _, n = scales.shape
    words = np.ascontiguousarray(words).reshape(g, 128, n, -1)
    if fmt == "e4m3":
        vals = words.view(ml_dtypes.float8_e4m3fn).astype(np.float64)
    else:
        nib = np.empty((g, 128, n, 4), np.uint8)
        nib[..., 0::2] = words & 0xF
        nib[..., 1::2] = words >> 4
        vals = E2M1[nib]
    vals = vals * np.repeat(np.exp2(scales.astype(np.float64) - 127.0), 8, axis=1)[..., None]
    return vals.transpose(0, 1, 3, 2).reshape(g * 512, n)


def relu(v):
    return np.maximum(v, 0.0)


def sigmoid(v):
    return 1.0 / (1.0 + np.exp(-np.maximum(v, -700.0)))


K, T, E, C, H, N = 1024, 512, 4, 128, 512, 256


def by_expert(wq, xq):
    return np.concatenate([wq[e].T @ xq[:, e * C:(e + 1) * C] for e in range(E)], axis=1)


def setup_inputs():
    n = np.random.standard_normal
    s = mx_kscale(K)
    u = mx_kscale(H)
    slot_token = np.random.permutation(T)[:E * C]
    x = pack_weight(n((K, T)) * s[:, None], "e4m3")
    w1 = [pack_weight(m, "e2m1") for m in n((E, K, H)) / np.sqrt(K) / s[None, :, None] * u]
    w2 = [pack_weight(m, "e2m1") for m in n((E, H, N)) / np.sqrt(H) / u[None, :, None]]
    return {
        "x_words": x[0],
        "x_scales": x[1],
        "wg": (n((K, N)) / np.sqrt(K) / s[:, None]).astype(np.float32),
        "w1_words": np.stack([m[0] for m in w1]),
        "w1_scales": np.stack([m[1] for m in w1]),
        "w2_words": np.stack([m[0] for m in w2]),
        "w2_scales": np.stack([m[1] for m in w2]),
        "gate": np.tile(np.random.uniform(0.2, 1.0, E * C), (128, 1)).astype(np.float32),
        "offs": striped(slot_token),
    }


def reference(x_words, x_scales, wg, w1_words, w1_scales, w2_words, w2_scales, gate, offs):
    wgq = mxq(f64(wg), 0, "e4m3")
    w1 = np.stack([unpack_weight(w1_words[e], w1_scales[e], "e2m1") for e in range(E)])
    w2 = np.stack([unpack_weight(w2_words[e], w2_scales[e], "e2m1") for e in range(E)])
    idx = unstriped(offs)
    x = unpack_weight(x_words, x_scales, "e4m3")
    o = sigmoid(wgq.T @ x)
    h = relu(by_expert(w1, x[:, idx]))
    y = by_expert(w2, mxq(h, 0, "e4m3"))
    c = np.zeros((N, T))
    c[:, idx] = f64(gate[:1]) * y
    return o * c

@@ -1,0 +1,230 @@
+from contextlib import ExitStack
+
+import concourse.mybir as mybir
+from concourse.masks import make_identity
+
+K, T, E, C, H, N = 1024, 512, 4, 128, 512, 256
+FLOPS = 2 * T * (K * N + K * H + H * N)
+
+F32 = mybir.dt.float32
+BF16 = mybir.dt.bfloat16
+I32 = mybir.dt.int32
+U32 = mybir.dt.uint32
+U16 = mybir.dt.uint16
+U8 = mybir.dt.uint8
+FP8X4 = mybir.dt.float8_e4m3fn_x4
+FP4X4 = mybir.dt.float4_e2m1fn_x4
+ACT = mybir.ActivationFunctionType
+MULT = mybir.AluOpType.mult
+
+P = 128
+PASSES = K // 512
+BLOCKS = N // P
+LIST_COLS = C // 16
+
+
+def load_scale_rows(queues, plane, rows):
+    for r in queues:
+        queues[r].dma_start(out=plane[r:P:32, :, :].bitcast(I32), in_=rows[r].bitcast(I32))
+
+
+def tile_moe_ogt_relu_sigmoid_kernel(
+    tc, x_words, x_scales, wg, w1_words, w1_scales, w2_words, w2_scales, gate, offs, out
+):
+    nc = tc.nc
+    with ExitStack() as ctx:
+        keep = ctx.enter_context(tc.tile_pool(name="keep", bufs=1))
+        psum = ctx.enter_context(tc.psum_pool(name="psum", bufs=2))
+
+        offsets = keep.tile([P, T // 16], U16, name="offsets")
+        xw = [keep.tile([P, T], I32, name=f"xw{s}", align_bytes=64) for s in range(PASSES)]
+        xs = keep.tile([P, PASSES, T], U8, name="xs", align_bytes=64)
+        w1s = keep.tile([P, E * PASSES, H], U8, name="w1s", align_bytes=64)
+        w2s = keep.tile([P, E, N], U8, name="w2s", align_bytes=64)
+        ident = keep.tile([P, P], F32, name="ident")
+        warm = keep.tile([P, 8], F32, name="warm")
+        warm_out = keep.tile([P, 8], F32, name="warm_out")
+        w1w = [keep.tile([P, PASSES, 2 * H], U8, name=f"w1w{e}", align_bytes=64) for e in range(E)]
+        w2w = keep.tile([P, E, 2 * N], U8, name="w2w", align_bytes=64)
+        wg_raw = {(b, s): keep.tile([P, 4, P], F32, name=f"wg_raw{b}{s}") for b in range(BLOCKS) for s in range(PASSES)}
+        gates = keep.tile([P, T], F32, name="gates")
+
+        def load_x(s):
+            nc.scalar.dma_start(out=xw[s][:], in_=x_words[s].rearrange("p t d -> p (t d)").bitcast(I32))
+
+        def load_w1(queue, e):
+            queue.dma_start(out=w1w[e][:].bitcast(I32), in_=w1_words[e].rearrange("s p b -> p s b").bitcast(I32))
+
+        def load_wg(b, s):
+            rows = wg[512 * s : 512 * (s + 1), P * b : P * (b + 1)]
+            nc.sync.dma_start(out=wg_raw[b, s][:], in_=rows.rearrange("(p j) n -> p j n", j=4))
+
+        nc.gpsimd.memset(xs[:].rearrange("p s t -> p (s t)").bitcast(I32), 0)
+        nc.vector.memset(w1s[:].rearrange("p m h -> p (m h)").bitcast(I32), 0)
+        nc.gpsimd.memset(w2s[:].rearrange("p e n -> p (e n)").bitcast(I32), 0)
+        nc.vector.memset(warm[:], 0.0)
+        make_identity(nc, ident[:])
+        nc.sync.dma_start(offsets[:], offs)
+        load_x(0)
+        load_scale_rows({0: nc.sync, 1: nc.sync, 2: nc.sync, 3: nc.scalar}, xs, x_scales.rearrange("s (q r) t -> r q s t", r=4))
+        load_w1(nc.scalar, 0)
+        load_x(1)
+        load_scale_rows({0: nc.sync, 1: nc.sync, 2: nc.scalar, 3: nc.scalar}, w1s, w1_scales.rearrange("e s (q r) h -> r q (e s) h", r=4))
+        nc.scalar.activation(out=warm_out[:], in_=warm[:], func=ACT.Sigmoid)
+        w2_rows = w2_scales.rearrange("e s (q r) n -> r q (e s) n", r=4)
+        load_scale_rows({0: nc.scalar, 1: nc.scalar}, w2s, w2_rows)
+        load_wg(1, 0)
+        load_wg(1, 1)
+        load_w1(nc.sync, 1)
+        load_w1(nc.sync, 2)
+        nc.sync.dma_start(out=w2w[:].bitcast(I32), in_=w2_words.rearrange("e s p b -> p (e s) b").bitcast(I32))
+        load_scale_rows({2: nc.sync}, w2s, w2_rows)
+        load_scale_rows({3: nc.sync}, w2s, w2_rows)
+        load_w1(nc.sync, 3)
+        nc.sync.dma_start(out=gates[:], in_=gate)
+        load_wg(0, 0)
+        load_wg(0, 1)
+
+        gw = [keep.tile([P, T], I32, name=f"gw{s}", align_bytes=64) for s in range(PASSES)]
+        gs = [keep.tile([P, T], U8, name=f"gs{s}", align_bytes=64) for s in range(PASSES)]
+        y = keep.tile([P, BLOCKS, T], F32, name="y")
+        result = [keep.tile([P, T], F32, name=f"result{b}") for b in range(BLOCKS)]
+
+        def slots(e):
+            return slice(e * C, (e + 1) * C)
+
+        def list_of(e):
+            return offsets[:, e * LIST_COLS : (e + 1) * LIST_COLS]
+
+        def gather(e):
+            for s in range(PASSES):
+                nc.vector.tensor_copy(gw[s][:, slots(e)].bitcast(U32), xw[s][:].bitcast(U32).indirect(list_of(e)))
+                nc.vector.tensor_copy(gs[s][:, slots(e)], xs[:, s, :].indirect(list_of(e)))
+
+        def first_layer(e):
+            acc = psum.tile([P, H], F32, name="h_acc")
+            for s in range(PASSES):
+                nc.tensor.matmul_mx(
+                    out=acc[:],
+                    lhsT=gw[s][:, slots(e)].bitcast(FP8X4),
+                    lhsT_scale=gs[s][:, slots(e)],
+                    rhs=w1w[e][:, s, :].bitcast(FP4X4),
+                    rhs_scale=w1s[:, e * PASSES + s, :],
+                    start=(s == 0),
+                    stop=(s == PASSES - 1),
+                )
+            h_rows = keep.tile([P, H], BF16, name=f"h_rows{e}", align_bytes=64)
+            nc.scalar.activation(
+                out=h_rows[:].rearrange("j (u p d) -> j u p d", u=2, d=2),
+                in_=acc[:].rearrange("j (p u d) -> j u p d", u=2, d=2),
+                func=ACT.Relu,
+            )
+            return h_rows
+
+        def quantise_hidden(e, h_rows):
+            turned = psum.tile([P, 2, C], F32, name="turned")
+            for u in range(2):
+                nc.tensor.transpose(turned[:, u, :], h_rows[:].bitcast(F32)[:, u * P : (u + 1) * P], ident[:])
+            h_cols = keep.tile([P, 4 * C], BF16, name=f"h_cols{e}", tag=f"h_cols{e}", align_bytes=64)
+            nc.scalar.copy(
+                out=h_cols[:].bitcast(F32).rearrange("p (j u) -> p j u", u=2),
+                in_=turned[:].rearrange("p u j -> p j u"),
+            )
+            h_q = keep.tile([P, C], U32, name=f"h_q{e}", align_bytes=64)
+            h_s = keep.tile([P, C], U8, name=f"h_s{e}", align_bytes=64)
+            nc.vector.quantize_mx(out=h_q[:].bitcast(FP8X4), scales=h_s[:], in_=h_cols[:])
+            return h_q, h_s
+
+        def second_layer(e, h_q, h_s):
+            acc = psum.tile([P, BLOCKS, C], F32, name="y_acc")
+            for b in range(BLOCKS):
+                nc.tensor.matmul_mx(
+                    out=acc[:, b, :],
+                    lhsT=w2w[:, e, 2 * P * b : 2 * P * (b + 1)].bitcast(FP4X4),
+                    lhsT_scale=w2s[:, e, P * b : P * (b + 1)],
+                    rhs=h_q[:].bitcast(FP8X4),
+                    rhs_scale=h_s[:],
+                    start=True,
+                    stop=True,
+                )
+            nc.scalar.copy(out=y[:, :, slots(e)], in_=acc[:])
+
+        def scatter(b, e, factor):
+            nc.vector.tensor_tensor(result[b][:].indirect(list_of(e)), y[:, b, slots(e)], factor, MULT)
+
+        wg_b = [keep.tile([P, PASSES, P, 4], BF16, name=f"wg_b{b}", tag=f"wg_b{b}", align_bytes=64) for b in range(BLOCKS)]
+        wg_q = {}
+        wg_s = [keep.tile([P, PASSES * P], U8, name=f"wg_s{b}", align_bytes=64) for b in range(BLOCKS)]
+
+        def round_wg(b, s):
+            nc.scalar.copy(
+                out=wg_b[b][:, s, :, :].rearrange("p (c i) j -> p c j i", i=4),
+                in_=wg_raw[b, s][:].rearrange("p j (c i) -> p c j i", i=4),
+            )
+
+        def quantise_wg(b, tag):
+            wg_q[b] = keep.tile([P, PASSES * P], U32, name=f"wg_q{b}", tag=tag, align_bytes=64)
+            nc.vector.quantize_mx(
+                out=wg_q[b][:].bitcast(FP8X4), scales=wg_s[b][:], in_=wg_b[b][:].rearrange("p s n j -> p (s n j)")
+            )
+
+        def gate_sums(b, words, scales):
+            acc = psum.tile([P, T], F32, name="o_acc")
+            for s in range(PASSES):
+                nc.tensor.matmul_mx(
+                    out=acc[:],
+                    lhsT=wg_q[b][:, P * s : P * (s + 1)].bitcast(FP8X4),
+                    lhsT_scale=wg_s[b][:, P * s : P * (s + 1)],
+                    rhs=words[s].bitcast(FP8X4),
+                    rhs_scale=scales[s],
+                    start=(s == 0),
+                    stop=(s == PASSES - 1),
+                )
+            return acc
+
+        def sigmoid(sums, name):
+            o = keep.tile([P, sums.shape[1]], F32, name=name)
+            nc.scalar.activation(out=o[:], in_=sums, func=ACT.Sigmoid)
+            return o
+
+        half = T // 2
+
+        def times_gate(h, o, tag):
+            og = keep.tile([P, half], F32, name=f"og{h}", tag=tag, align_bytes=64)
+            nc.vector.tensor_tensor(out=og[:], in0=o[:], in1=gates[:, h * half : (h + 1) * half], op=MULT)
+            return og
+
+        for e in range(E):
+            gather(e)
+        round_wg(1, 0)
+        round_wg(1, 1)
+        codes0 = quantise_hidden(0, first_layer(0))
+        codes1 = quantise_hidden(1, first_layer(1))
+        second_layer(0, *codes0)
+        scatter(0, 0, gates[:, slots(0)])
+        quantise_wg(1, "h_cols0")
+        slot_sums = gate_sums(1, [gw[s][:] for s in range(PASSES)], [gs[s][:] for s in range(PASSES)])
+        codes2 = quantise_hidden(2, first_layer(2))
+        second_layer(1, *codes1)
+        scatter(0, 1, gates[:, slots(1)])
+        codes3 = quantise_hidden(3, first_layer(3))
+        og0 = times_gate(0, sigmoid(slot_sums[:, :half], "o_first"), "og0")
+        scatter(1, 0, og0[:, :C])
+        scatter(1, 1, og0[:, C:])
+        second_layer(2, *codes2)
+        scatter(0, 2, gates[:, slots(2)])
+        second_layer(3, *codes3)
+        o_second = sigmoid(slot_sums[:, half:], "o_second")
+        round_wg(0, 0)
+        round_wg(0, 1)
+        quantise_wg(0, "wg_q0")
+        token_sums = gate_sums(0, [xw[s][:] for s in range(PASSES)], [xs[:, s, :] for s in range(PASSES)])
+        o_tokens = sigmoid(token_sums[:], "o_tokens")
+        og1 = times_gate(1, o_second, "wg_b0")
+        scatter(1, 2, og1[:, :C])
+        scatter(0, 3, gates[:, slots(3)])
+        scatter(1, 3, og1[:, C:])
+        nc.sync.dma_start(out=out[P:, :], in_=result[1][:])
+        gated = keep.tile([P, T], F32, name="gated")
+        nc.vector.tensor_tensor(out=gated[:], in0=result[0][:], in1=o_tokens[:], op=MULT)
+        nc.sync.dma_start(out=out[:P, :], in_=gated[:])

@@ -34,7 +34,7 @@ def tile_moe_ogt_relu_sigmoid_kernel(
     nc = tc.nc
     with ExitStack() as ctx:
         keep = ctx.enter_context(tc.tile_pool(name="keep", bufs=1))
-        psum = ctx.enter_context(tc.psum_pool(name="psum", bufs=2))
+        psum = ctx.enter_context(tc.psum_pool(name="psum", bufs=1))
 
         offsets = keep.tile([P, T // 16], U16, name="offsets")
         xw = [keep.tile([P, T], I32, name=f"xw{s}", align_bytes=64) for s in range(PASSES)]
@@ -72,13 +72,12 @@ def tile_moe_ogt_relu_sigmoid_kernel(
         load_scale_rows({0: nc.sync, 1: nc.sync, 2: nc.scalar, 3: nc.scalar}, w1s, w1_scales.rearrange("e s (q r) h -> r q (e s) h", r=4))
         nc.scalar.activation(out=warm_out[:], in_=warm[:], func=ACT.Sigmoid)
         w2_rows = w2_scales.rearrange("e s (q r) n -> r q (e s) n", r=4)
-        load_scale_rows({0: nc.scalar, 1: nc.scalar}, w2s, w2_rows)
+        load_scale_rows({0: nc.scalar, 1: nc.scalar, 2: nc.scalar}, w2s, w2_rows)
         load_wg(1, 0)
-        load_wg(1, 1)
         load_w1(nc.sync, 1)
+        load_wg(1, 1)
         load_w1(nc.sync, 2)
         nc.sync.dma_start(out=w2w[:].bitcast(I32), in_=w2_words.rearrange("e s p b -> p (e s) b").bitcast(I32))
-        load_scale_rows({2: nc.sync}, w2s, w2_rows)
         load_scale_rows({3: nc.sync}, w2s, w2_rows)
         load_w1(nc.sync, 3)
         nc.sync.dma_start(out=gates[:], in_=gate)
@@ -96,13 +95,16 @@ def tile_moe_ogt_relu_sigmoid_kernel(
         def list_of(e):
             return offsets[:, e * LIST_COLS : (e + 1) * LIST_COLS]
 
-        def gather(e):
-            for s in range(PASSES):
-                nc.vector.tensor_copy(gw[s][:, slots(e)].bitcast(U32), xw[s][:].bitcast(U32).indirect(list_of(e)))
-                nc.vector.tensor_copy(gs[s][:, slots(e)], xs[:, s, :].indirect(list_of(e)))
+        def gather_words(s, first, count):
+            cols = slice(first * C, (first + count) * C)
+            entries = offsets[:, first * LIST_COLS : (first + count) * LIST_COLS]
+            nc.vector.tensor_copy(gw[s][:, cols].bitcast(U32), xw[s][:].bitcast(U32).indirect(entries))
+
+        def gather_scales(s, e):
+            nc.vector.tensor_copy(gs[s][:, slots(e)], xs[:, s, :].indirect(list_of(e)))
 
         def first_layer(e):
-            acc = psum.tile([P, H], F32, name="h_acc")
+            acc = psum.tile([P, H], F32, name="h_acc", tag=f"h_acc{e % 2}")
             for s in range(PASSES):
                 nc.tensor.matmul_mx(
                     out=acc[:],
@@ -113,7 +115,7 @@ def tile_moe_ogt_relu_sigmoid_kernel(
                     start=(s == 0),
                     stop=(s == PASSES - 1),
                 )
-            h_rows = keep.tile([P, H], BF16, name=f"h_rows{e}", align_bytes=64)
+            h_rows = keep.tile([P, H], BF16, name=f"h_rows{e}", tag=f"h_rows{e}", align_bytes=64)
             nc.scalar.activation(
                 out=h_rows[:].rearrange("j (u p d) -> j u p d", u=2, d=2),
                 in_=acc[:].rearrange("j (p u d) -> j u p d", u=2, d=2),
@@ -122,7 +124,7 @@ def tile_moe_ogt_relu_sigmoid_kernel(
             return h_rows
 
         def quantise_hidden(e, h_rows):
-            turned = psum.tile([P, 2, C], F32, name="turned")
+            turned = psum.tile([P, 2, C], F32, name="turned", tag=f"turned{e}")
             for u in range(2):
                 nc.tensor.transpose(turned[:, u, :], h_rows[:].bitcast(F32)[:, u * P : (u + 1) * P], ident[:])
             h_cols = keep.tile([P, 4 * C], BF16, name=f"h_cols{e}", tag=f"h_cols{e}", align_bytes=64)
@@ -136,7 +138,7 @@ def tile_moe_ogt_relu_sigmoid_kernel(
             return h_q, h_s
 
         def second_layer(e, h_q, h_s):
-            acc = psum.tile([P, BLOCKS, C], F32, name="y_acc")
+            acc = psum.tile([P, BLOCKS, C], F32, name="y_acc", tag=f"y_acc{e % 2}")
             for b in range(BLOCKS):
                 nc.tensor.matmul_mx(
                     out=acc[:, b, :],
@@ -149,10 +151,12 @@ def tile_moe_ogt_relu_sigmoid_kernel(
                 )
             nc.scalar.copy(out=y[:, :, slots(e)], in_=acc[:])
 
-        def scatter(b, e, factor):
-            nc.vector.tensor_tensor(result[b][:].indirect(list_of(e)), y[:, b, slots(e)], factor, MULT)
+        def scatter(b, first, count, factor):
+            entries = offsets[:, first * LIST_COLS : (first + count) * LIST_COLS]
+            values = y[:, b, first * C : (first + count) * C]
+            nc.vector.tensor_tensor(result[b][:].indirect(entries), values, factor, MULT)
 
-        wg_b = [keep.tile([P, PASSES, P, 4], BF16, name=f"wg_b{b}", tag=f"wg_b{b}", align_bytes=64) for b in range(BLOCKS)]
+        wg_b = {1: keep.tile([P, PASSES, P, 4], BF16, name="wg_b1", align_bytes=64)}
         wg_q = {}
         wg_s = [keep.tile([P, PASSES * P], U8, name=f"wg_s{b}", align_bytes=64) for b in range(BLOCKS)]
 
@@ -168,8 +172,8 @@ def tile_moe_ogt_relu_sigmoid_kernel(
                 out=wg_q[b][:].bitcast(FP8X4), scales=wg_s[b][:], in_=wg_b[b][:].rearrange("p s n j -> p (s n j)")
             )
 
-        def gate_sums(b, words, scales):
-            acc = psum.tile([P, T], F32, name="o_acc")
+        def gate_sums(b, words, scales, bank):
+            acc = psum.tile([P, T], F32, name="o_acc", tag=bank)
             for s in range(PASSES):
                 nc.tensor.matmul_mx(
                     out=acc[:],
@@ -195,35 +199,39 @@ def tile_moe_ogt_relu_sigmoid_kernel(
             return og
 
         for e in range(E):
-            gather(e)
+            if e % 2 == 0:
+                gather_words(0, e, 2)
+            gather_scales(0, e)
+            gather_words(1, e, 1)
+            gather_scales(1, e)
         round_wg(1, 0)
+        rows0 = first_layer(0)
         round_wg(1, 1)
-        codes0 = quantise_hidden(0, first_layer(0))
+        second_layer(0, *quantise_hidden(0, rows0))
         codes1 = quantise_hidden(1, first_layer(1))
-        second_layer(0, *codes0)
-        scatter(0, 0, gates[:, slots(0)])
-        quantise_wg(1, "h_cols0")
-        slot_sums = gate_sums(1, [gw[s][:] for s in range(PASSES)], [gs[s][:] for s in range(PASSES)])
-        codes2 = quantise_hidden(2, first_layer(2))
+        quantise_wg(1, "wg_q1")
+        scatter(0, 0, 1, gates[:, slots(0)])
         second_layer(1, *codes1)
-        scatter(0, 1, gates[:, slots(1)])
+        codes2 = quantise_hidden(2, first_layer(2))
         codes3 = quantise_hidden(3, first_layer(3))
+        slot_sums = gate_sums(1, [gw[s][:] for s in range(PASSES)], [gs[s][:] for s in range(PASSES)], "turned1")
+        scatter(0, 1, 1, gates[:, slots(1)])
         og0 = times_gate(0, sigmoid(slot_sums[:, :half], "o_first"), "og0")
-        scatter(1, 0, og0[:, :C])
-        scatter(1, 1, og0[:, C:])
         second_layer(2, *codes2)
-        scatter(0, 2, gates[:, slots(2)])
+        scatter(1, 0, 1, og0[:, :C])
+        scatter(0, 2, 1, gates[:, slots(2)])
+        scatter(1, 1, 1, og0[:, C:])
         second_layer(3, *codes3)
         o_second = sigmoid(slot_sums[:, half:], "o_second")
+        wg_b[0] = keep.tile([P, PASSES, P, 4], BF16, name="wg_b0", tag="h_rows3", align_bytes=64)
         round_wg(0, 0)
         round_wg(0, 1)
         quantise_wg(0, "wg_q0")
-        token_sums = gate_sums(0, [xw[s][:] for s in range(PASSES)], [xs[:, s, :] for s in range(PASSES)])
+        token_sums = gate_sums(0, [xw[s][:] for s in range(PASSES)], [xs[:, s, :] for s in range(PASSES)], "turned0")
         o_tokens = sigmoid(token_sums[:], "o_tokens")
-        og1 = times_gate(1, o_second, "wg_b0")
-        scatter(1, 2, og1[:, :C])
-        scatter(0, 3, gates[:, slots(3)])
-        scatter(1, 3, og1[:, C:])
+        og1 = times_gate(1, o_second, "og1")
+        scatter(0, 3, 1, gates[:, slots(3)])
+        scatter(1, 2, 2, og1[:])
         nc.sync.dma_start(out=out[P:, :], in_=result[1][:])
         gated = keep.tile([P, T], F32, name="gated")
         nc.vector.tensor_tensor(out=gated[:], in0=result[0][:], in1=o_tokens[:], op=MULT)

@@ -198,6 +198,17 @@ def tile_moe_ogt_relu_sigmoid_kernel(
             nc.vector.tensor_tensor(out=og[:], in0=o[:], in1=gates[:, h * half : (h + 1) * half], op=MULT)
             return og
 
+        idle = psum.tile([P, T], F32, name="idle", tag="y_acc1")
+        for turn_no in range(3):
+            nc.tensor.matmul_mx(
+                out=idle[:],
+                lhsT=xw[0][:][:, :P].bitcast(FP8X4),
+                lhsT_scale=xs[:, 0, :][:, :P],
+                rhs=xw[0][:].bitcast(FP8X4),
+                rhs_scale=xs[:, 0, :],
+                start=True,
+                stop=True,
+            )
         for e in range(E):
             if e % 2 == 0:
                 gather_words(0, e, 2)

@@ -44,7 +44,7 @@ def tile_moe_ogt_relu_sigmoid_kernel(
         ident = keep.tile([P, P], F32, name="ident")
         warm = keep.tile([P, 8], F32, name="warm")
         warm_out = keep.tile([P, 8], F32, name="warm_out")
-        w1w = [keep.tile([P, PASSES, 2 * H], U8, name=f"w1w{e}", align_bytes=64) for e in range(E)]
+        w1w = [keep.tile([P, PASSES, 2 * H], U8, name=f"w1w{e}", tag=f"w1w{e}", align_bytes=64) for e in range(E)]
         w2w = keep.tile([P, E, 2 * N], U8, name="w2w", align_bytes=64)
         wg_raw = {(b, s): keep.tile([P, 4, P], F32, name=f"wg_raw{b}{s}") for b in range(BLOCKS) for s in range(PASSES)}
         gates = keep.tile([P, T], F32, name="gates")
@@ -59,7 +59,7 @@ def tile_moe_ogt_relu_sigmoid_kernel(
             rows = wg[512 * s : 512 * (s + 1), P * b : P * (b + 1)]
             nc.sync.dma_start(out=wg_raw[b, s][:], in_=rows.rearrange("(p j) n -> p j n", j=4))
 
-        nc.gpsimd.memset(xs[:].rearrange("p s t -> p (s t)").bitcast(I32), 0)
+        nc.vector.memset(xs[:].rearrange("p s t -> p (s t)").bitcast(I32), 0)
         nc.vector.memset(w1s[:].rearrange("p m h -> p (m h)").bitcast(I32), 0)
         nc.gpsimd.memset(w2s[:].rearrange("p e n -> p (e n)").bitcast(I32), 0)
         nc.vector.memset(warm[:], 0.0)
@@ -67,8 +67,8 @@ def tile_moe_ogt_relu_sigmoid_kernel(
         nc.sync.dma_start(offsets[:], offs)
         load_x(0)
         load_scale_rows({0: nc.sync, 1: nc.sync, 2: nc.sync, 3: nc.scalar}, xs, x_scales.rearrange("s (q r) t -> r q s t", r=4))
-        load_w1(nc.scalar, 0)
         load_x(1)
+        load_w1(nc.scalar, 0)
         load_scale_rows({0: nc.sync, 1: nc.sync, 2: nc.scalar, 3: nc.scalar}, w1s, w1_scales.rearrange("e s (q r) h -> r q (e s) h", r=4))
         nc.scalar.activation(out=warm_out[:], in_=warm[:], func=ACT.Sigmoid)
         w2_rows = w2_scales.rearrange("e s (q r) n -> r q (e s) n", r=4)
@@ -79,37 +79,36 @@ def tile_moe_ogt_relu_sigmoid_kernel(
         load_w1(nc.sync, 2)
         nc.sync.dma_start(out=w2w[:].bitcast(I32), in_=w2_words.rearrange("e s p b -> p (e s) b").bitcast(I32))
         load_scale_rows({3: nc.sync}, w2s, w2_rows)
-        load_w1(nc.sync, 3)
         nc.sync.dma_start(out=gates[:], in_=gate)
+        load_w1(nc.sync, 3)
         load_wg(0, 0)
         load_wg(0, 1)
 
-        gw = [keep.tile([P, T], I32, name=f"gw{s}", align_bytes=64) for s in range(PASSES)]
-        gs = [keep.tile([P, T], U8, name=f"gs{s}", align_bytes=64) for s in range(PASSES)]
+        gw = {(s, 0): keep.tile([P, T // 2], I32, name=f"gw{s}0", align_bytes=64)[:] for s in range(PASSES)}
+        gs = {(s, h): keep.tile([P, T // 2], U8, name=f"gs{s}{h}", align_bytes=64) for s in range(PASSES) for h in range(2)}
         y = keep.tile([P, BLOCKS, T], F32, name="y")
         result = [keep.tile([P, T], F32, name=f"result{b}") for b in range(BLOCKS)]
 
         def slots(e):
             return slice(e * C, (e + 1) * C)
 
-        def list_of(e):
-            return offsets[:, e * LIST_COLS : (e + 1) * LIST_COLS]
-
         def gather_words(s, first, count):
-            cols = slice(first * C, (first + count) * C)
+            cols = slice(first % 2 * C, (first % 2 + count) * C)
             entries = offsets[:, first * LIST_COLS : (first + count) * LIST_COLS]
-            nc.vector.tensor_copy(gw[s][:, cols].bitcast(U32), xw[s][:].bitcast(U32).indirect(entries))
+            nc.vector.tensor_copy(gw[s, first // 2][:, cols].bitcast(U32), xw[s][:].bitcast(U32).indirect(entries))
 
-        def gather_scales(s, e):
-            nc.vector.tensor_copy(gs[s][:, slots(e)], xs[:, s, :].indirect(list_of(e)))
+        def gather_scales(s, first, count):
+            cols = slice(first % 2 * C, (first % 2 + count) * C)
+            entries = offsets[:, first * LIST_COLS : (first + count) * LIST_COLS]
+            nc.vector.tensor_copy(gs[s, first // 2][:, cols], xs[:, s, :].indirect(entries))
 
         def first_layer(e):
             acc = psum.tile([P, H], F32, name="h_acc", tag=f"h_acc{e % 2}")
             for s in range(PASSES):
                 nc.tensor.matmul_mx(
                     out=acc[:],
-                    lhsT=gw[s][:, slots(e)].bitcast(FP8X4),
-                    lhsT_scale=gs[s][:, slots(e)],
+                    lhsT=gw[s, e // 2][:, slots(e % 2)].bitcast(FP8X4),
+                    lhsT_scale=gs[s, e // 2][:, slots(e % 2)],
                     rhs=w1w[e][:, s, :].bitcast(FP4X4),
                     rhs_scale=w1s[:, e * PASSES + s, :],
                     start=(s == 0),
@@ -137,7 +136,7 @@ def tile_moe_ogt_relu_sigmoid_kernel(
             nc.vector.quantize_mx(out=h_q[:].bitcast(FP8X4), scales=h_s[:], in_=h_cols[:])
             return h_q, h_s
 
-        def second_layer(e, h_q, h_s):
+        def second_layer(e, h_q, h_s, parts=(slice(0, BLOCKS),)):
             acc = psum.tile([P, BLOCKS, C], F32, name="y_acc", tag=f"y_acc{e % 2}")
             for b in range(BLOCKS):
                 nc.tensor.matmul_mx(
@@ -149,7 +148,8 @@ def tile_moe_ogt_relu_sigmoid_kernel(
                     start=True,
                     stop=True,
                 )
-            nc.scalar.copy(out=y[:, :, slots(e)], in_=acc[:])
+            for part in parts:
+                nc.scalar.copy(out=y[:, part, slots(e)], in_=acc[:, part, :])
 
         def scatter(b, first, count, factor):
             entries = offsets[:, first * LIST_COLS : (first + count) * LIST_COLS]
@@ -172,11 +172,10 @@ def tile_moe_ogt_relu_sigmoid_kernel(
                 out=wg_q[b][:].bitcast(FP8X4), scales=wg_s[b][:], in_=wg_b[b][:].rearrange("p s n j -> p (s n j)")
             )
 
-        def gate_sums(b, words, scales, bank):
-            acc = psum.tile([P, T], F32, name="o_acc", tag=bank)
+        def gate_sums(b, words, scales, acc):
             for s in range(PASSES):
                 nc.tensor.matmul_mx(
-                    out=acc[:],
+                    out=acc,
                     lhsT=wg_q[b][:, P * s : P * (s + 1)].bitcast(FP8X4),
                     lhsT_scale=wg_s[b][:, P * s : P * (s + 1)],
                     rhs=words[s].bitcast(FP8X4),
@@ -184,7 +183,6 @@ def tile_moe_ogt_relu_sigmoid_kernel(
                     start=(s == 0),
                     stop=(s == PASSES - 1),
                 )
-            return acc
 
         def sigmoid(sums, name):
             o = keep.tile([P, sums.shape[1]], F32, name=name)
@@ -209,23 +207,30 @@ def tile_moe_ogt_relu_sigmoid_kernel(
                 start=True,
                 stop=True,
             )
-        for e in range(E):
-            if e % 2 == 0:
-                gather_words(0, e, 2)
-            gather_scales(0, e)
-            gather_words(1, e, 1)
-            gather_scales(1, e)
+        gather_words(0, 0, 2)
+        gather_words(1, 0, 2)
+        for first, count in ((0, 1), (1, 1), (2, 2)):
+            gather_scales(0, first, count)
+            gather_scales(1, first, count)
         round_wg(1, 0)
         rows0 = first_layer(0)
         round_wg(1, 1)
-        second_layer(0, *quantise_hidden(0, rows0))
+        codes0 = quantise_hidden(0, rows0)
+        late_words = keep.tile([P, PASSES, T // 2], I32, name="late_words", tag="w1w0", align_bytes=64)
+        for s in range(PASSES):
+            gw[s, 1] = late_words[:, s, :]
+            gather_words(s, 2, 2)
+        second_layer(0, *codes0, parts=(slice(0, 1), slice(1, 2)))
         codes1 = quantise_hidden(1, first_layer(1))
         quantise_wg(1, "wg_q1")
         scatter(0, 0, 1, gates[:, slots(0)])
         second_layer(1, *codes1)
         codes2 = quantise_hidden(2, first_layer(2))
         codes3 = quantise_hidden(3, first_layer(3))
-        slot_sums = gate_sums(1, [gw[s][:] for s in range(PASSES)], [gs[s][:] for s in range(PASSES)], "turned1")
+        slot_sums = psum.tile([P, T], F32, name="slot_sums", tag="turned1")
+        for h in range(2):
+            cols = slice(h * half, (h + 1) * half)
+            gate_sums(1, [gw[s, h] for s in range(PASSES)], [gs[s, h][:] for s in range(PASSES)], slot_sums[:, cols])
         scatter(0, 1, 1, gates[:, slots(1)])
         og0 = times_gate(0, sigmoid(slot_sums[:, :half], "o_first"), "og0")
         second_layer(2, *codes2)
@@ -238,8 +243,12 @@ def tile_moe_ogt_relu_sigmoid_kernel(
         round_wg(0, 0)
         round_wg(0, 1)
         quantise_wg(0, "wg_q0")
-        token_sums = gate_sums(0, [xw[s][:] for s in range(PASSES)], [xs[:, s, :] for s in range(PASSES)], "turned0")
-        o_tokens = sigmoid(token_sums[:], "o_tokens")
+        o_tokens = keep.tile([P, T], F32, name="o_tokens")
+        for h, bank in enumerate(("turned0", "turned2")):
+            cols = slice(h * half, (h + 1) * half)
+            token_sums = psum.tile([P, half], F32, name="token_sums", tag=bank)
+            gate_sums(0, [xw[s][:, cols] for s in range(PASSES)], [xs[:, s, cols] for s in range(PASSES)], token_sums[:])
+            nc.scalar.activation(out=o_tokens[:, cols], in_=token_sums[:], func=ACT.Sigmoid)
         og1 = times_gate(1, o_second, "og1")
         scatter(0, 3, 1, gates[:, slots(3)])
         scatter(1, 2, 2, og1[:])

@@ -72,15 +72,16 @@ def tile_moe_ogt_relu_sigmoid_kernel(
         load_scale_rows({0: nc.sync, 1: nc.sync, 2: nc.scalar, 3: nc.scalar}, w1s, w1_scales.rearrange("e s (q r) h -> r q (e s) h", r=4))
         nc.scalar.activation(out=warm_out[:], in_=warm[:], func=ACT.Sigmoid)
         w2_rows = w2_scales.rearrange("e s (q r) n -> r q (e s) n", r=4)
-        load_scale_rows({0: nc.scalar, 1: nc.scalar, 2: nc.scalar}, w2s, w2_rows)
+        load_w1(nc.scalar, 2)
+        load_scale_rows({1: nc.scalar, 2: nc.scalar}, w2s, w2_rows)
         load_wg(1, 0)
         load_w1(nc.sync, 1)
         load_wg(1, 1)
-        load_w1(nc.sync, 2)
+        load_scale_rows({0: nc.sync}, w2s, w2_rows)
         nc.sync.dma_start(out=w2w[:].bitcast(I32), in_=w2_words.rearrange("e s p b -> p (e s) b").bitcast(I32))
         load_scale_rows({3: nc.sync}, w2s, w2_rows)
-        nc.sync.dma_start(out=gates[:], in_=gate)
         load_w1(nc.sync, 3)
+        nc.sync.dma_start(out=gates[:], in_=gate)
         load_wg(0, 0)
         load_wg(0, 1)
 
@@ -156,12 +157,12 @@ def tile_moe_ogt_relu_sigmoid_kernel(
             values = y[:, b, first * C : (first + count) * C]
             nc.vector.tensor_tensor(result[b][:].indirect(entries), values, factor, MULT)
 
-        wg_b = {1: keep.tile([P, PASSES, P, 4], BF16, name="wg_b1", align_bytes=64)}
+        wg_b = {}
         wg_q = {}
         wg_s = [keep.tile([P, PASSES * P], U8, name=f"wg_s{b}", align_bytes=64) for b in range(BLOCKS)]
 
-        def round_wg(b, s):
-            nc.scalar.copy(
+        def round_wg(copy, b, s):
+            copy(
                 out=wg_b[b][:, s, :, :].rearrange("p (c i) j -> p c j i", i=4),
                 in_=wg_raw[b, s][:].rearrange("p j (c i) -> p c j i", i=4),
             )
@@ -212,9 +213,9 @@ def tile_moe_ogt_relu_sigmoid_kernel(
         for first, count in ((0, 1), (1, 1), (2, 2)):
             gather_scales(0, first, count)
             gather_scales(1, first, count)
-        round_wg(1, 0)
         rows0 = first_layer(0)
-        round_wg(1, 1)
+        wg_b[1] = keep.tile([P, PASSES, P, 4], BF16, name="wg_b1", align_bytes=64)
+        round_wg(nc.scalar.copy, 1, 0)
         codes0 = quantise_hidden(0, rows0)
         late_words = keep.tile([P, PASSES, T // 2], I32, name="late_words", tag="w1w0", align_bytes=64)
         for s in range(PASSES):
@@ -222,7 +223,8 @@ def tile_moe_ogt_relu_sigmoid_kernel(
             gather_words(s, 2, 2)
         second_layer(0, *codes0, parts=(slice(0, 1), slice(1, 2)))
         codes1 = quantise_hidden(1, first_layer(1))
-        quantise_wg(1, "wg_q1")
+        round_wg(nc.vector.tensor_copy, 1, 1)
+        quantise_wg(1, "h_cols0")
         scatter(0, 0, 1, gates[:, slots(0)])
         second_layer(1, *codes1)
         codes2 = quantise_hidden(2, first_layer(2))
@@ -240,8 +242,8 @@ def tile_moe_ogt_relu_sigmoid_kernel(
         second_layer(3, *codes3)
         o_second = sigmoid(slot_sums[:, half:], "o_second")
         wg_b[0] = keep.tile([P, PASSES, P, 4], BF16, name="wg_b0", tag="h_rows3", align_bytes=64)
-        round_wg(0, 0)
-        round_wg(0, 1)
+        round_wg(nc.scalar.copy, 0, 0)
+        round_wg(nc.scalar.copy, 0, 1)
         quantise_wg(0, "wg_q0")
         o_tokens = keep.tile([P, T], F32, name="o_tokens")
         for h, bank in enumerate(("turned0", "turned2")):

@@ -1,7 +1,6 @@
 from contextlib import ExitStack
 
 import concourse.mybir as mybir
-from concourse.masks import make_identity
 
 K, T, E, C, H, N = 1024, 512, 4, 128, 512, 256
 FLOPS = 2 * T * (K * N + K * H + H * N)
@@ -15,17 +14,38 @@ U8 = mybir.dt.uint8
 FP8X4 = mybir.dt.float8_e4m3fn_x4
 FP4X4 = mybir.dt.float4_e2m1fn_x4
 ACT = mybir.ActivationFunctionType
-MULT = mybir.AluOpType.mult
+ALU = mybir.AluOpType
+MULT = ALU.mult
 
 P = 128
 PASSES = K // 512
 BLOCKS = N // P
 LIST_COLS = C // 16
+PAIR = 2 * C
 
 
 def load_scale_rows(queues, plane, rows):
     for r in queues:
         queues[r].dma_start(out=plane[r:P:32, :, :].bitcast(I32), in_=rows[r].bitcast(I32))
+
+
+def build_identity(nc, pool, ident):
+    ones = pool.tile([P, P], F32, name="ones")
+    column = pool.tile([P, P], F32, name="column", align_bytes=64)
+    row_in_quadrant = pool.tile([P, 32], F32, name="row_in_quadrant", align_bytes=64)
+    nc.vector.memset(ones[:], 1.0)
+    nc.vector.tensor_tensor_scan(out=column[:], data0=ones[:], data1=ones[:], initial=0.0, op0=MULT, op1=ALU.add)
+    nc.vector.transpose(out=row_in_quadrant[:], in_=column[:, :32])
+    for q in range(4):
+        rows = slice(32 * q, 32 * (q + 1))
+        nc.vector.tensor_scalar(
+            out=ident[rows, :],
+            in0=column[rows, :],
+            scalar1=row_in_quadrant[rows, 0:1],
+            scalar2=float(32 * q),
+            op0=ALU.subtract,
+            op1=ALU.is_equal,
+        )
 
 
 def tile_moe_ogt_relu_sigmoid_kernel(
@@ -34,7 +54,11 @@ def tile_moe_ogt_relu_sigmoid_kernel(
     nc = tc.nc
     with ExitStack() as ctx:
         keep = ctx.enter_context(tc.tile_pool(name="keep", bufs=1))
+        shared = ctx.enter_context(tc.tile_pool(name="shared", bufs=1))
         psum = ctx.enter_context(tc.psum_pool(name="psum", bufs=1))
+
+        def reused(name, shape, dtype, place):
+            return shared.tile(shape, dtype, name=name, offset=place * 512, align_bytes=64)
 
         offsets = keep.tile([P, T // 16], U16, name="offsets")
         xw = [keep.tile([P, T], I32, name=f"xw{s}", align_bytes=64) for s in range(PASSES)]
@@ -44,78 +68,83 @@ def tile_moe_ogt_relu_sigmoid_kernel(
         ident = keep.tile([P, P], F32, name="ident")
         warm = keep.tile([P, 8], F32, name="warm")
         warm_out = keep.tile([P, 8], F32, name="warm_out")
-        w1w = [keep.tile([P, PASSES, 2 * H], U8, name=f"w1w{e}", tag=f"w1w{e}", align_bytes=64) for e in range(E)]
-        w2w = keep.tile([P, E, 2 * N], U8, name="w2w", align_bytes=64)
-        wg_raw = {(b, s): keep.tile([P, 4, P], F32, name=f"wg_raw{b}{s}") for b in range(BLOCKS) for s in range(PASSES)}
+        w1_first = shared.tile([P, PASSES, 2 * H], U8, name="w1_first", offset=0, align_bytes=64)
+        w1_rest = [keep.tile([P, PASSES, 2 * H], U8, name=f"w1w{e}", tag=f"w1w{e}", align_bytes=64) for e in range(1, E)]
+        w1w = [w1_first[:]] + [w[:] for w in w1_rest]
+        w2w = [keep.tile([P, 2, 2 * N], U8, name=f"w2w{pair}", align_bytes=64) for pair in range(2)]
+        wg_first = reused("wg_first", [P, 4, N], F32, 4)
+        wg_second = [keep.tile([P, 4, P], F32, name=f"wg_second{b}") for b in range(BLOCKS)]
         gates = keep.tile([P, T], F32, name="gates")
 
         def load_x(s):
             nc.scalar.dma_start(out=xw[s][:], in_=x_words[s].rearrange("p t d -> p (t d)").bitcast(I32))
 
         def load_w1(queue, e):
-            queue.dma_start(out=w1w[e][:].bitcast(I32), in_=w1_words[e].rearrange("s p b -> p s b").bitcast(I32))
+            queue.dma_start(out=w1w[e].bitcast(I32), in_=w1_words[e].rearrange("s p b -> p s b").bitcast(I32))
 
-        def load_wg(b, s):
-            rows = wg[512 * s : 512 * (s + 1), P * b : P * (b + 1)]
-            nc.sync.dma_start(out=wg_raw[b, s][:], in_=rows.rearrange("(p j) n -> p j n", j=4))
+        def load_w2(pair):
+            words = w2_words[2 * pair : 2 * pair + 2].rearrange("e s p b -> p (e s) b")
+            nc.sync.dma_start(out=w2w[pair][:].bitcast(I32), in_=words.bitcast(I32))
+
+        def load_wg(raw, rows):
+            nc.sync.dma_start(out=raw[:], in_=rows.rearrange("(p j) n -> p j n", j=4))
 
         nc.vector.memset(xs[:].rearrange("p s t -> p (s t)").bitcast(I32), 0)
-        nc.vector.memset(w1s[:].rearrange("p m h -> p (m h)").bitcast(I32), 0)
-        nc.gpsimd.memset(w2s[:].rearrange("p e n -> p (e n)").bitcast(I32), 0)
         nc.vector.memset(warm[:], 0.0)
-        make_identity(nc, ident[:])
+        nc.vector.memset(w1s[:].rearrange("p m h -> p (m h)").bitcast(I32), 0)
+        build_identity(nc, keep, ident)
+        nc.gpsimd.memset(w2s[:].rearrange("p e n -> p (e n)").bitcast(I32), 0)
         nc.sync.dma_start(offsets[:], offs)
         load_x(0)
         load_scale_rows({0: nc.sync, 1: nc.sync, 2: nc.sync, 3: nc.scalar}, xs, x_scales.rearrange("s (q r) t -> r q s t", r=4))
         load_x(1)
         load_w1(nc.scalar, 0)
         load_scale_rows({0: nc.sync, 1: nc.sync, 2: nc.scalar, 3: nc.scalar}, w1s, w1_scales.rearrange("e s (q r) h -> r q (e s) h", r=4))
-        nc.scalar.activation(out=warm_out[:], in_=warm[:], func=ACT.Sigmoid)
         w2_rows = w2_scales.rearrange("e s (q r) n -> r q (e s) n", r=4)
-        load_w1(nc.scalar, 2)
-        load_scale_rows({1: nc.scalar, 2: nc.scalar}, w2s, w2_rows)
-        load_wg(1, 0)
+        load_scale_rows({0: nc.scalar}, w2s, w2_rows)
+        nc.scalar.activation(out=warm_out[:], in_=warm[:], func=ACT.Sigmoid)
+        load_scale_rows({1: nc.scalar, 2: nc.scalar, 3: nc.scalar}, w2s, w2_rows)
+        load_wg(wg_first, wg[:512, :])
         load_w1(nc.sync, 1)
-        load_wg(1, 1)
-        load_scale_rows({0: nc.sync}, w2s, w2_rows)
-        nc.sync.dma_start(out=w2w[:].bitcast(I32), in_=w2_words.rearrange("e s p b -> p (e s) b").bitcast(I32))
-        load_scale_rows({3: nc.sync}, w2s, w2_rows)
+        load_wg(wg_second[1], wg[512:, P:])
+        load_w2(0)
+        load_w1(nc.sync, 2)
         load_w1(nc.sync, 3)
         nc.sync.dma_start(out=gates[:], in_=gate)
-        load_wg(0, 0)
-        load_wg(0, 1)
+        load_wg(wg_second[0], wg[512:, :P])
+        load_w2(1)
 
-        gw = {(s, 0): keep.tile([P, T // 2], I32, name=f"gw{s}0", align_bytes=64)[:] for s in range(PASSES)}
-        gs = {(s, h): keep.tile([P, T // 2], U8, name=f"gs{s}{h}", align_bytes=64) for s in range(PASSES) for h in range(2)}
-        y = keep.tile([P, BLOCKS, T], F32, name="y")
-        result = [keep.tile([P, T], F32, name=f"result{b}") for b in range(BLOCKS)]
+        early_words = [keep.tile([P, PAIR], I32, name=f"early_words{s}", align_bytes=64) for s in range(PASSES)]
+        gw = {(s, e): early_words[s][:, e * C : (e + 1) * C] for s in range(PASSES) for e in range(2)}
+        gs = {(s, h): keep.tile([P, PAIR], U8, name=f"gs{s}{h}", align_bytes=64) for s in range(PASSES) for h in range(2)}
+        result = {}
 
         def slots(e):
             return slice(e * C, (e + 1) * C)
 
-        def gather_words(s, first, count):
-            cols = slice(first % 2 * C, (first % 2 + count) * C)
-            entries = offsets[:, first * LIST_COLS : (first + count) * LIST_COLS]
-            nc.vector.tensor_copy(gw[s, first // 2][:, cols].bitcast(U32), xw[s][:].bitcast(U32).indirect(entries))
+        def entries(first, count=1):
+            return offsets[:, first * LIST_COLS : (first + count) * LIST_COLS]
+
+        def gather_words(words, s, first, count):
+            nc.vector.tensor_copy(words.bitcast(U32), xw[s][:].bitcast(U32).indirect(entries(first, count)))
 
         def gather_scales(s, first, count):
             cols = slice(first % 2 * C, (first % 2 + count) * C)
-            entries = offsets[:, first * LIST_COLS : (first + count) * LIST_COLS]
-            nc.vector.tensor_copy(gs[s, first // 2][:, cols], xs[:, s, :].indirect(entries))
+            nc.vector.tensor_copy(gs[s, first // 2][:, cols], xs[:, s, :].indirect(entries(first, count)))
 
         def first_layer(e):
-            acc = psum.tile([P, H], F32, name="h_acc", tag=f"h_acc{e % 2}")
+            acc = psum.tile([P, H], F32, name="h_acc", tag=f"bank{(0, 1, 4, 5)[e]}")
             for s in range(PASSES):
                 nc.tensor.matmul_mx(
                     out=acc[:],
-                    lhsT=gw[s, e // 2][:, slots(e % 2)].bitcast(FP8X4),
+                    lhsT=gw[s, e].bitcast(FP8X4),
                     lhsT_scale=gs[s, e // 2][:, slots(e % 2)],
                     rhs=w1w[e][:, s, :].bitcast(FP4X4),
                     rhs_scale=w1s[:, e * PASSES + s, :],
                     start=(s == 0),
                     stop=(s == PASSES - 1),
                 )
-            h_rows = keep.tile([P, H], BF16, name=f"h_rows{e}", tag=f"h_rows{e}", align_bytes=64)
+            h_rows = reused(f"h_rows{e}", [P, H], BF16, (4, 9, 15, 39)[e])
             nc.scalar.activation(
                 out=h_rows[:].rearrange("j (u p d) -> j u p d", u=2, d=2),
                 in_=acc[:].rearrange("j (p u d) -> j u p d", u=2, d=2),
@@ -123,137 +152,132 @@ def tile_moe_ogt_relu_sigmoid_kernel(
             )
             return h_rows
 
-        def quantise_hidden(e, h_rows):
-            turned = psum.tile([P, 2, C], F32, name="turned", tag=f"turned{e}")
-            for u in range(2):
-                nc.tensor.transpose(turned[:, u, :], h_rows[:].bitcast(F32)[:, u * P : (u + 1) * P], ident[:])
-            h_cols = keep.tile([P, 4 * C], BF16, name=f"h_cols{e}", tag=f"h_cols{e}", align_bytes=64)
-            nc.scalar.copy(
+        def quantise_hidden(first, h_rows, bank, copy):
+            count = len(h_rows)
+            turned = psum.tile([P, 2, count, C], F32, name="turned", tag=bank)
+            for i in range(count):
+                for u in range(2):
+                    nc.tensor.transpose(turned[:, u, i, :], h_rows[i][:].bitcast(F32)[:, u * P : (u + 1) * P], ident[:])
+            h_cols = reused(f"h_cols{first}", [P, 4 * count * C], BF16, (32, 19, 21, 13)[first])
+            copy(
                 out=h_cols[:].bitcast(F32).rearrange("p (j u) -> p j u", u=2),
-                in_=turned[:].rearrange("p u j -> p j u"),
+                in_=turned[:].rearrange("p u i j -> p (i j) u"),
             )
-            h_q = keep.tile([P, C], U32, name=f"h_q{e}", align_bytes=64)
-            h_s = keep.tile([P, C], U8, name=f"h_s{e}", align_bytes=64)
+            h_q = keep.tile([P, count * C], U32, name=f"h_q{first}", align_bytes=64)
+            h_s = keep.tile([P, count * C], U8, name=f"h_s{first}", align_bytes=64)
             nc.vector.quantize_mx(out=h_q[:].bitcast(FP8X4), scales=h_s[:], in_=h_cols[:])
             return h_q, h_s
 
-        def second_layer(e, h_q, h_s, parts=(slice(0, BLOCKS),)):
-            acc = psum.tile([P, BLOCKS, C], F32, name="y_acc", tag=f"y_acc{e % 2}")
-            for b in range(BLOCKS):
-                nc.tensor.matmul_mx(
-                    out=acc[:, b, :],
-                    lhsT=w2w[:, e, 2 * P * b : 2 * P * (b + 1)].bitcast(FP4X4),
-                    lhsT_scale=w2s[:, e, P * b : P * (b + 1)],
-                    rhs=h_q[:].bitcast(FP8X4),
-                    rhs_scale=h_s[:],
-                    start=True,
-                    stop=True,
-                )
-            for part in parts:
-                nc.scalar.copy(out=y[:, part, slots(e)], in_=acc[:, part, :])
+        def second_layer(first, count, codes, bank):
+            h_q, h_s = codes
+            acc = psum.tile([P, BLOCKS, count * C], F32, name="y_acc", tag=bank)
+            for i in range(count):
+                for b in range(BLOCKS):
+                    nc.tensor.matmul_mx(
+                        out=acc[:, b, slots(i)],
+                        lhsT=w2w[(first + i) // 2][:, (first + i) % 2, 2 * P * b : 2 * P * (b + 1)].bitcast(FP4X4),
+                        lhsT_scale=w2s[:, first + i, P * b : P * (b + 1)],
+                        rhs=h_q[:, slots(i)].bitcast(FP8X4),
+                        rhs_scale=h_s[:, slots(i)],
+                        start=True,
+                        stop=True,
+                    )
+            return acc
 
-        def scatter(b, first, count, factor):
-            entries = offsets[:, first * LIST_COLS : (first + count) * LIST_COLS]
-            values = y[:, b, first * C : (first + count) * C]
-            nc.vector.tensor_tensor(result[b][:].indirect(entries), values, factor, MULT)
+        def times_weight(y, sums, first, count):
+            weight = gates[:, first * C : (first + count) * C].unsqueeze(1).to_broadcast([P, BLOCKS, count * C])
+            nc.vector.tensor_tensor(out=y, in0=sums, in1=weight, op=MULT)
 
-        wg_b = {}
-        wg_q = {}
+        def scatter_plain(y, first, count):
+            nc.scalar.activation(out=result[0][:].indirect(entries(first, count)), in_=y[:, 0, :], func=ACT.Copy)
+
+        def scatter_gated(y, first, count, o):
+            nc.vector.tensor_tensor(result[1][:].indirect(entries(first, count)), y[:, 1, :], o, MULT)
+
+        wg_b = keep.tile([P, BLOCKS, PASSES, P, 4], BF16, name="wg_b", align_bytes=64)
+        wg_q = {1: keep.tile([P, PASSES * P], U32, name="wg_q1", align_bytes=64)}
         wg_s = [keep.tile([P, PASSES * P], U8, name=f"wg_s{b}", align_bytes=64) for b in range(BLOCKS)]
 
-        def round_wg(copy, b, s):
-            copy(
-                out=wg_b[b][:, s, :, :].rearrange("p (c i) j -> p c j i", i=4),
-                in_=wg_raw[b, s][:].rearrange("p j (c i) -> p c j i", i=4),
+        def round_second_pass(b):
+            nc.vector.tensor_copy(
+                out=wg_b[:, b, 1, :, :].rearrange("p (c i) j -> p c j i", i=4),
+                in_=wg_second[b][:].rearrange("p j (c i) -> p c j i", i=4),
             )
 
-        def quantise_wg(b, tag):
-            wg_q[b] = keep.tile([P, PASSES * P], U32, name=f"wg_q{b}", tag=tag, align_bytes=64)
+        def quantise_wg(b):
             nc.vector.quantize_mx(
-                out=wg_q[b][:].bitcast(FP8X4), scales=wg_s[b][:], in_=wg_b[b][:].rearrange("p s n j -> p (s n j)")
+                out=wg_q[b][:].bitcast(FP8X4), scales=wg_s[b][:], in_=wg_b[:, b].rearrange("p s n j -> p (s n j)")
             )
 
-        def gate_sums(b, words, scales, acc):
-            for s in range(PASSES):
-                nc.tensor.matmul_mx(
-                    out=acc,
-                    lhsT=wg_q[b][:, P * s : P * (s + 1)].bitcast(FP8X4),
-                    lhsT_scale=wg_s[b][:, P * s : P * (s + 1)],
-                    rhs=words[s].bitcast(FP8X4),
-                    rhs_scale=scales[s],
-                    start=(s == 0),
-                    stop=(s == PASSES - 1),
-                )
-
-        def sigmoid(sums, name):
-            o = keep.tile([P, sums.shape[1]], F32, name=name)
-            nc.scalar.activation(out=o[:], in_=sums, func=ACT.Sigmoid)
+        def output_gate(b, parts, bank, o):
+            width = sum(words[0].shape[1] for words, scales in parts)
+            sums = psum.tile([P, width], F32, name="gate_sums", tag=bank)
+            first = 0
+            for words, scales in parts:
+                cols = slice(first, first + words[0].shape[1])
+                first = cols.stop
+                for s in range(PASSES):
+                    nc.tensor.matmul_mx(
+                        out=sums[:, cols],
+                        lhsT=wg_q[b][:, P * s : P * (s + 1)].bitcast(FP8X4),
+                        lhsT_scale=wg_s[b][:, P * s : P * (s + 1)],
+                        rhs=words[s].bitcast(FP8X4),
+                        rhs_scale=scales[s],
+                        start=(s == 0),
+                        stop=(s == PASSES - 1),
+                    )
+            nc.scalar.activation(out=o[:], in_=sums[:], func=ACT.Sigmoid)
             return o
 
-        half = T // 2
-
-        def times_gate(h, o, tag):
-            og = keep.tile([P, half], F32, name=f"og{h}", tag=tag, align_bytes=64)
-            nc.vector.tensor_tensor(out=og[:], in0=o[:], in1=gates[:, h * half : (h + 1) * half], op=MULT)
-            return og
-
-        idle = psum.tile([P, T], F32, name="idle", tag="y_acc1")
-        for turn_no in range(3):
-            nc.tensor.matmul_mx(
-                out=idle[:],
-                lhsT=xw[0][:][:, :P].bitcast(FP8X4),
-                lhsT_scale=xs[:, 0, :][:, :P],
-                rhs=xw[0][:].bitcast(FP8X4),
-                rhs_scale=xs[:, 0, :],
-                start=True,
-                stop=True,
-            )
-        gather_words(0, 0, 2)
-        gather_words(1, 0, 2)
-        for first, count in ((0, 1), (1, 1), (2, 2)):
-            gather_scales(0, first, count)
-            gather_scales(1, first, count)
-        rows0 = first_layer(0)
-        wg_b[1] = keep.tile([P, PASSES, P, 4], BF16, name="wg_b1", align_bytes=64)
-        round_wg(nc.scalar.copy, 1, 0)
-        codes0 = quantise_hidden(0, rows0)
-        late_words = keep.tile([P, PASSES, T // 2], I32, name="late_words", tag="w1w0", align_bytes=64)
         for s in range(PASSES):
-            gw[s, 1] = late_words[:, s, :]
-            gather_words(s, 2, 2)
-        second_layer(0, *codes0, parts=(slice(0, 1), slice(1, 2)))
-        codes1 = quantise_hidden(1, first_layer(1))
-        round_wg(nc.vector.tensor_copy, 1, 1)
-        quantise_wg(1, "h_cols0")
-        scatter(0, 0, 1, gates[:, slots(0)])
-        second_layer(1, *codes1)
-        codes2 = quantise_hidden(2, first_layer(2))
-        codes3 = quantise_hidden(3, first_layer(3))
-        slot_sums = psum.tile([P, T], F32, name="slot_sums", tag="turned1")
-        for h in range(2):
-            cols = slice(h * half, (h + 1) * half)
-            gate_sums(1, [gw[s, h] for s in range(PASSES)], [gs[s, h][:] for s in range(PASSES)], slot_sums[:, cols])
-        scatter(0, 1, 1, gates[:, slots(1)])
-        og0 = times_gate(0, sigmoid(slot_sums[:, :half], "o_first"), "og0")
-        second_layer(2, *codes2)
-        scatter(1, 0, 1, og0[:, :C])
-        scatter(0, 2, 1, gates[:, slots(2)])
-        scatter(1, 1, 1, og0[:, C:])
-        second_layer(3, *codes3)
-        o_second = sigmoid(slot_sums[:, half:], "o_second")
-        wg_b[0] = keep.tile([P, PASSES, P, 4], BF16, name="wg_b0", tag="h_rows3", align_bytes=64)
-        round_wg(nc.scalar.copy, 0, 0)
-        round_wg(nc.scalar.copy, 0, 1)
-        quantise_wg(0, "wg_q0")
-        o_tokens = keep.tile([P, T], F32, name="o_tokens")
-        for h, bank in enumerate(("turned0", "turned2")):
-            cols = slice(h * half, (h + 1) * half)
-            token_sums = psum.tile([P, half], F32, name="token_sums", tag=bank)
-            gate_sums(0, [xw[s][:, cols] for s in range(PASSES)], [xs[:, s, cols] for s in range(PASSES)], token_sums[:])
-            nc.scalar.activation(out=o_tokens[:, cols], in_=token_sums[:], func=ACT.Sigmoid)
-        og1 = times_gate(1, o_second, "og1")
-        scatter(0, 3, 1, gates[:, slots(3)])
-        scatter(1, 2, 2, og1[:])
+            gather_words(early_words[s][:], s, 0, 2)
+        for first, count in ((0, 2), (2, 2)):
+            for s in range(PASSES):
+                gather_scales(s, first, count)
+        nc.scalar.copy(
+            out=wg_b[:, :, 0, :, :].rearrange("p b (c i) j -> p b c j i", i=4),
+            in_=wg_first[:].rearrange("p j (b c i) -> p b c j i", b=BLOCKS, i=4),
+        )
+        rows0 = first_layer(0)
+        late_words = [reused(f"late_words{s}", [P, PAIR], I32, 2 * s) for s in range(PASSES)]
+        gather_words(late_words[0][:], 0, 2, 2)
+        for e in (2, 3):
+            gather_words(late_words[1][:, slots(e - 2)], 1, e, 1)
+            for s in range(PASSES):
+                gw[s, e] = late_words[s][:, slots(e - 2)]
+        round_second_pass(1)
+        quantise_wg(1)
+        rows1 = first_layer(1)
+        codes0 = quantise_hidden(0, [rows0], "bank2", nc.scalar.copy)
+        codes1 = quantise_hidden(1, [rows1], "bank3", nc.vector.tensor_copy)
+        y = [keep.tile([P, BLOCKS, C], F32, name=f"y{e}") for e in range(2)]
+        times_weight(y[0][:], second_layer(0, 1, codes0, "bank6")[:], 0, 1)
+        rows2 = first_layer(2)
+        early_part = ([early_words[s][:] for s in range(PASSES)], [gs[s, 0][:] for s in range(PASSES)])
+        o_first = output_gate(1, [early_part], "bank2", keep.tile([P, PAIR], F32, name="o_first"))
+        rows3 = first_layer(3)
+        result[1] = keep.tile([P, T], F32, name="result1")
+        scatter_gated(y[0], 0, 1, o_first[:, slots(0)])
+        times_weight(y[1][:], second_layer(1, 1, codes1, "bank7")[:], 1, 1)
+        codes2 = quantise_hidden(2, [rows2], "bank0", nc.scalar.copy)
+        codes3 = quantise_hidden(3, [rows3], "bank1", nc.scalar.copy)
+        round_second_pass(0)
+        wg_q[0] = keep.tile([P, PASSES * P], U32, name="wg_q0", align_bytes=64)
+        quantise_wg(0)
+        result[0] = reused("result0", [P, T], F32, 36)
+        scatter_plain(y[0], 0, 1)
+        late_parts = [([w[:] for w in late_words], [gs[s, 1][:] for s in range(PASSES)])]
+        o_second = output_gate(1, late_parts, "bank6", reused("o_second", [P, PAIR], F32, 40))
+        scatter_gated(y[1], 1, 1, o_first[:, slots(1)])
+        scatter_plain(y[1], 1, 1)
+        y23 = reused("y23", [P, BLOCKS, PAIR], F32, 11)
+        times_weight(y23[:, :, slots(0)], second_layer(2, 1, codes2, "bank2")[:], 2, 1)
+        times_weight(y23[:, :, slots(1)], second_layer(3, 1, codes3, "bank3")[:], 3, 1)
+        tokens = ([xw[s][:] for s in range(PASSES)], [xs[:, s, :] for s in range(PASSES)])
+        o_tokens = output_gate(0, [tokens], "bank0", keep.tile([P, T], F32, name="o_tokens"))
+        for e in (2, 3):
+            scatter_plain(y23[:, :, slots(e - 2)], e, 1)
+        scatter_gated(y23, 2, 2, o_second[:])
         nc.sync.dma_start(out=out[P:, :], in_=result[1][:])
         gated = keep.tile([P, T], F32, name="gated")
         nc.vector.tensor_tensor(out=gated[:], in0=result[0][:], in1=o_tokens[:], op=MULT)

@@ -92,8 +92,8 @@ def tile_moe_ogt_relu_sigmoid_kernel(
         nc.vector.memset(xs[:].rearrange("p s t -> p (s t)").bitcast(I32), 0)
         nc.vector.memset(warm[:], 0.0)
         nc.vector.memset(w1s[:].rearrange("p m h -> p (m h)").bitcast(I32), 0)
+        nc.vector.memset(w2s[:].rearrange("p e n -> p (e n)").bitcast(I32), 0)
         build_identity(nc, keep, ident)
-        nc.gpsimd.memset(w2s[:].rearrange("p e n -> p (e n)").bitcast(I32), 0)
         nc.sync.dma_start(offsets[:], offs)
         load_x(0)
         load_scale_rows({0: nc.sync, 1: nc.sync, 2: nc.sync, 3: nc.scalar}, xs, x_scales.rearrange("s (q r) t -> r q s t", r=4))
@@ -152,17 +152,16 @@ def tile_moe_ogt_relu_sigmoid_kernel(
             )
             return h_rows
 
-        def quantise_hidden(first, h_rows, bank, copy):
-            count = len(h_rows)
-            turned = psum.tile([P, 2, count, C], F32, name="turned", tag=bank)
-            for i in range(count):
-                for u in range(2):
-                    nc.tensor.transpose(turned[:, u, i, :], h_rows[i][:].bitcast(F32)[:, u * P : (u + 1) * P], ident[:])
-            h_cols = reused(f"h_cols{first}", [P, 4 * count * C], BF16, (32, 19, 21, 13)[first])
+        def turn_hidden(h_cols, h_rows, bank, copy):
+            turned = psum.tile([P, 2, C], F32, name="turned", tag=bank)
+            for u in range(2):
+                nc.tensor.transpose(turned[:, u, :], h_rows[:].bitcast(F32)[:, u * P : (u + 1) * P], ident[:])
             copy(
-                out=h_cols[:].bitcast(F32).rearrange("p (j u) -> p j u", u=2),
-                in_=turned[:].rearrange("p u i j -> p (i j) u"),
+                out=h_cols.bitcast(F32).rearrange("p (j u) -> p j u", u=2),
+                in_=turned[:].rearrange("p u j -> p j u"),
             )
+
+        def quantise_hidden(first, count, h_cols):
             h_q = keep.tile([P, count * C], U32, name=f"h_q{first}", align_bytes=64)
             h_s = keep.tile([P, count * C], U8, name=f"h_s{first}", align_bytes=64)
             nc.vector.quantize_mx(out=h_q[:].bitcast(FP8X4), scales=h_s[:], in_=h_cols[:])
@@ -240,16 +239,19 @@ def tile_moe_ogt_relu_sigmoid_kernel(
         )
         rows0 = first_layer(0)
         late_words = [reused(f"late_words{s}", [P, PAIR], I32, 2 * s) for s in range(PASSES)]
-        gather_words(late_words[0][:], 0, 2, 2)
         for e in (2, 3):
-            gather_words(late_words[1][:, slots(e - 2)], 1, e, 1)
             for s in range(PASSES):
+                gather_words(late_words[s][:, slots(e - 2)], s, e, 1)
                 gw[s, e] = late_words[s][:, slots(e - 2)]
         round_second_pass(1)
         quantise_wg(1)
         rows1 = first_layer(1)
-        codes0 = quantise_hidden(0, [rows0], "bank2", nc.scalar.copy)
-        codes1 = quantise_hidden(1, [rows1], "bank3", nc.vector.tensor_copy)
+        cols0 = keep.tile([P, H], BF16, name="cols0", align_bytes=64)
+        turn_hidden(cols0[:], rows0, "bank2", nc.vector.tensor_copy)
+        codes0 = quantise_hidden(0, 1, cols0)
+        cols1 = keep.tile([P, H], BF16, name="cols1", align_bytes=64)
+        turn_hidden(cols1[:], rows1, "bank3", nc.scalar.copy)
+        codes1 = quantise_hidden(1, 1, cols1)
         y = [keep.tile([P, BLOCKS, C], F32, name=f"y{e}") for e in range(2)]
         times_weight(y[0][:], second_layer(0, 1, codes0, "bank6")[:], 0, 1)
         rows2 = first_layer(2)
@@ -259,8 +261,10 @@ def tile_moe_ogt_relu_sigmoid_kernel(
         result[1] = keep.tile([P, T], F32, name="result1")
         scatter_gated(y[0], 0, 1, o_first[:, slots(0)])
         times_weight(y[1][:], second_layer(1, 1, codes1, "bank7")[:], 1, 1)
-        codes2 = quantise_hidden(2, [rows2], "bank0", nc.scalar.copy)
-        codes3 = quantise_hidden(3, [rows3], "bank1", nc.scalar.copy)
+        cols23 = keep.tile([P, 2 * H], BF16, name="cols23", align_bytes=64)
+        turn_hidden(cols23[:, :H], rows2, "bank0", nc.scalar.copy)
+        turn_hidden(cols23[:, H:], rows3, "bank1", nc.scalar.copy)
+        codes23 = quantise_hidden(2, 2, cols23)
         round_second_pass(0)
         wg_q[0] = keep.tile([P, PASSES * P], U32, name="wg_q0", align_bytes=64)
         quantise_wg(0)
@@ -270,13 +274,11 @@ def tile_moe_ogt_relu_sigmoid_kernel(
         o_second = output_gate(1, late_parts, "bank6", reused("o_second", [P, PAIR], F32, 40))
         scatter_gated(y[1], 1, 1, o_first[:, slots(1)])
         scatter_plain(y[1], 1, 1)
-        y23 = reused("y23", [P, BLOCKS, PAIR], F32, 11)
-        times_weight(y23[:, :, slots(0)], second_layer(2, 1, codes2, "bank2")[:], 2, 1)
-        times_weight(y23[:, :, slots(1)], second_layer(3, 1, codes3, "bank3")[:], 3, 1)
+        y23 = keep.tile([P, BLOCKS, PAIR], F32, name="y23")
+        times_weight(y23[:], second_layer(2, 2, codes23, "bank2")[:], 2, 2)
         tokens = ([xw[s][:] for s in range(PASSES)], [xs[:, s, :] for s in range(PASSES)])
         o_tokens = output_gate(0, [tokens], "bank0", keep.tile([P, T], F32, name="o_tokens"))
-        for e in (2, 3):
-            scatter_plain(y23[:, :, slots(e - 2)], e, 1)
+        scatter_plain(y23, 2, 2)
         scatter_gated(y23, 2, 2, o_second[:])
         nc.sync.dma_start(out=out[P:, :], in_=result[1][:])
         gated = keep.tile([P, T], F32, name="gated")

@@ -250,7 +250,7 @@ def tile_moe_ogt_relu_sigmoid_kernel(
         turn_hidden(cols0[:], rows0, "bank2", nc.vector.tensor_copy)
         codes0 = quantise_hidden(0, 1, cols0)
         cols1 = keep.tile([P, H], BF16, name="cols1", align_bytes=64)
-        turn_hidden(cols1[:], rows1, "bank3", nc.scalar.copy)
+        turn_hidden(cols1[:], rows1, "bank3", nc.vector.tensor_copy)
         codes1 = quantise_hidden(1, 1, cols1)
         y = [keep.tile([P, BLOCKS, C], F32, name=f"y{e}") for e in range(2)]
         times_weight(y[0][:], second_layer(0, 1, codes0, "bank6")[:], 0, 1)

from contextlib import ExitStack

import concourse.mybir as mybir

K, T, E, C, H, N = 1024, 512, 4, 128, 512, 256
FLOPS = 2 * T * (K * N + K * H + H * N)

F32 = mybir.dt.float32
BF16 = mybir.dt.bfloat16
I32 = mybir.dt.int32
U32 = mybir.dt.uint32
U16 = mybir.dt.uint16
U8 = mybir.dt.uint8
FP8X4 = mybir.dt.float8_e4m3fn_x4
FP4X4 = mybir.dt.float4_e2m1fn_x4
ACT = mybir.ActivationFunctionType
ALU = mybir.AluOpType
MULT = ALU.mult

P = 128
PASSES = K // 512
BLOCKS = N // P
LIST_COLS = C // 16
PAIR = 2 * C


def load_scale_rows(queues, plane, rows):
    for r in queues:
        queues[r].dma_start(out=plane[r:P:32, :, :].bitcast(I32), in_=rows[r].bitcast(I32))


def build_identity(nc, pool, ident):
    ones = pool.tile([P, P], F32, name="ones")
    column = pool.tile([P, P], F32, name="column", align_bytes=64)
    row_in_quadrant = pool.tile([P, 32], F32, name="row_in_quadrant", align_bytes=64)
    nc.vector.memset(ones[:], 1.0)
    nc.vector.tensor_tensor_scan(out=column[:], data0=ones[:], data1=ones[:], initial=0.0, op0=MULT, op1=ALU.add)
    nc.vector.transpose(out=row_in_quadrant[:], in_=column[:, :32])
    for q in range(4):
        rows = slice(32 * q, 32 * (q + 1))
        nc.vector.tensor_scalar(
            out=ident[rows, :],
            in0=column[rows, :],
            scalar1=row_in_quadrant[rows, 0:1],
            scalar2=float(32 * q),
            op0=ALU.subtract,
            op1=ALU.is_equal,
        )


def tile_moe_ogt_relu_sigmoid_kernel(
    tc, x_words, x_scales, wg, w1_words, w1_scales, w2_words, w2_scales, gate, offs, out
):
    nc = tc.nc
    with ExitStack() as ctx:
        keep = ctx.enter_context(tc.tile_pool(name="keep", bufs=1))
        shared = ctx.enter_context(tc.tile_pool(name="shared", bufs=1))
        psum = ctx.enter_context(tc.psum_pool(name="psum", bufs=1))

        def reused(name, shape, dtype, place):
            return shared.tile(shape, dtype, name=name, offset=place * 512, align_bytes=64)

        offsets = keep.tile([P, T // 16], U16, name="offsets")
        xw = [keep.tile([P, T], I32, name=f"xw{s}", align_bytes=64) for s in range(PASSES)]
        xs = keep.tile([P, PASSES, T], U8, name="xs", align_bytes=64)
        w1s = keep.tile([P, E * PASSES, H], U8, name="w1s", align_bytes=64)
        w2s = keep.tile([P, E, N], U8, name="w2s", align_bytes=64)
        ident = keep.tile([P, P], F32, name="ident")
        warm = keep.tile([P, 8], F32, name="warm")
        warm_out = keep.tile([P, 8], F32, name="warm_out")
        w1_first = shared.tile([P, PASSES, 2 * H], U8, name="w1_first", offset=0, align_bytes=64)
        w1_rest = [keep.tile([P, PASSES, 2 * H], U8, name=f"w1w{e}", tag=f"w1w{e}", align_bytes=64) for e in range(1, E)]
        w1w = [w1_first[:]] + [w[:] for w in w1_rest]
        w2w = [keep.tile([P, 2, 2 * N], U8, name=f"w2w{pair}", align_bytes=64) for pair in range(2)]
        wg_first = reused("wg_first", [P, 4, N], F32, 4)
        wg_second = [keep.tile([P, 4, P], F32, name=f"wg_second{b}") for b in range(BLOCKS)]
        gates = keep.tile([P, T], F32, name="gates")

        def load_x(s):
            nc.scalar.dma_start(out=xw[s][:], in_=x_words[s].rearrange("p t d -> p (t d)").bitcast(I32))

        def load_w1(queue, e):
            queue.dma_start(out=w1w[e].bitcast(I32), in_=w1_words[e].rearrange("s p b -> p s b").bitcast(I32))

        def load_w2(pair):
            words = w2_words[2 * pair : 2 * pair + 2].rearrange("e s p b -> p (e s) b")
            nc.sync.dma_start(out=w2w[pair][:].bitcast(I32), in_=words.bitcast(I32))

        def load_wg(raw, rows):
            nc.sync.dma_start(out=raw[:], in_=rows.rearrange("(p j) n -> p j n", j=4))

        nc.vector.memset(xs[:].rearrange("p s t -> p (s t)").bitcast(I32), 0)
        nc.vector.memset(warm[:], 0.0)
        nc.vector.memset(w1s[:].rearrange("p m h -> p (m h)").bitcast(I32), 0)
        nc.vector.memset(w2s[:].rearrange("p e n -> p (e n)").bitcast(I32), 0)
        build_identity(nc, keep, ident)
        nc.sync.dma_start(offsets[:], offs)
        load_x(0)
        load_scale_rows({0: nc.sync, 1: nc.sync, 2: nc.sync, 3: nc.scalar}, xs, x_scales.rearrange("s (q r) t -> r q s t", r=4))
        load_x(1)
        load_w1(nc.scalar, 0)
        load_scale_rows({0: nc.sync, 1: nc.sync, 2: nc.scalar, 3: nc.scalar}, w1s, w1_scales.rearrange("e s (q r) h -> r q (e s) h", r=4))
        w2_rows = w2_scales.rearrange("e s (q r) n -> r q (e s) n", r=4)
        load_scale_rows({0: nc.scalar}, w2s, w2_rows)
        nc.scalar.activation(out=warm_out[:], in_=warm[:], func=ACT.Sigmoid)
        load_scale_rows({1: nc.scalar, 2: nc.scalar, 3: nc.scalar}, w2s, w2_rows)
        load_wg(wg_first, wg[:512, :])
        load_w1(nc.sync, 1)
        load_wg(wg_second[1], wg[512:, P:])
        load_w2(0)
        load_w1(nc.sync, 2)
        load_w1(nc.sync, 3)
        nc.sync.dma_start(out=gates[:], in_=gate)
        load_wg(wg_second[0], wg[512:, :P])
        load_w2(1)

        early_words = [keep.tile([P, PAIR], I32, name=f"early_words{s}", align_bytes=64) for s in range(PASSES)]
        gw = {(s, e): early_words[s][:, e * C : (e + 1) * C] for s in range(PASSES) for e in range(2)}
        gs = {(s, h): keep.tile([P, PAIR], U8, name=f"gs{s}{h}", align_bytes=64) for s in range(PASSES) for h in range(2)}
        result = {}

        def slots(e):
            return slice(e * C, (e + 1) * C)

        def entries(first, count=1):
            return offsets[:, first * LIST_COLS : (first + count) * LIST_COLS]

        def gather_words(words, s, first, count):
            nc.vector.tensor_copy(words.bitcast(U32), xw[s][:].bitcast(U32).indirect(entries(first, count)))

        def gather_scales(s, first, count):
            cols = slice(first % 2 * C, (first % 2 + count) * C)
            nc.vector.tensor_copy(gs[s, first // 2][:, cols], xs[:, s, :].indirect(entries(first, count)))

        def first_layer(e):
            acc = psum.tile([P, H], F32, name="h_acc", tag=f"bank{(0, 1, 4, 5)[e]}")
            for s in range(PASSES):
                nc.tensor.matmul_mx(
                    out=acc[:],
                    lhsT=gw[s, e].bitcast(FP8X4),
                    lhsT_scale=gs[s, e // 2][:, slots(e % 2)],
                    rhs=w1w[e][:, s, :].bitcast(FP4X4),
                    rhs_scale=w1s[:, e * PASSES + s, :],
                    start=(s == 0),
                    stop=(s == PASSES - 1),
                )
            h_rows = reused(f"h_rows{e}", [P, H], BF16, (4, 9, 15, 39)[e])
            nc.scalar.activation(
                out=h_rows[:].rearrange("j (u p d) -> j u p d", u=2, d=2),
                in_=acc[:].rearrange("j (p u d) -> j u p d", u=2, d=2),
                func=ACT.Relu,
            )
            return h_rows

        def turn_hidden(h_cols, h_rows, bank, copy):
            turned = psum.tile([P, 2, C], F32, name="turned", tag=bank)
            for u in range(2):
                nc.tensor.transpose(turned[:, u, :], h_rows[:].bitcast(F32)[:, u * P : (u + 1) * P], ident[:])
            copy(
                out=h_cols.bitcast(F32).rearrange("p (j u) -> p j u", u=2),
                in_=turned[:].rearrange("p u j -> p j u"),
            )

        def quantise_hidden(first, count, h_cols):
            h_q = keep.tile([P, count * C], U32, name=f"h_q{first}", align_bytes=64)
            h_s = keep.tile([P, count * C], U8, name=f"h_s{first}", align_bytes=64)
            nc.vector.quantize_mx(out=h_q[:].bitcast(FP8X4), scales=h_s[:], in_=h_cols[:])
            return h_q, h_s

        def second_layer(first, count, codes, bank):
            h_q, h_s = codes
            acc = psum.tile([P, BLOCKS, count * C], F32, name="y_acc", tag=bank)
            for i in range(count):
                for b in range(BLOCKS):
                    nc.tensor.matmul_mx(
                        out=acc[:, b, slots(i)],
                        lhsT=w2w[(first + i) // 2][:, (first + i) % 2, 2 * P * b : 2 * P * (b + 1)].bitcast(FP4X4),
                        lhsT_scale=w2s[:, first + i, P * b : P * (b + 1)],
                        rhs=h_q[:, slots(i)].bitcast(FP8X4),
                        rhs_scale=h_s[:, slots(i)],
                        start=True,
                        stop=True,
                    )
            return acc

        def times_weight(y, sums, first, count):
            weight = gates[:, first * C : (first + count) * C].unsqueeze(1).to_broadcast([P, BLOCKS, count * C])
            nc.vector.tensor_tensor(out=y, in0=sums, in1=weight, op=MULT)

        def scatter_plain(y, first, count):
            nc.scalar.activation(out=result[0][:].indirect(entries(first, count)), in_=y[:, 0, :], func=ACT.Copy)

        def scatter_gated(y, first, count, o):
            nc.vector.tensor_tensor(result[1][:].indirect(entries(first, count)), y[:, 1, :], o, MULT)

        wg_b = keep.tile([P, BLOCKS, PASSES, P, 4], BF16, name="wg_b", align_bytes=64)
        wg_q = {1: keep.tile([P, PASSES * P], U32, name="wg_q1", align_bytes=64)}
        wg_s = [keep.tile([P, PASSES * P], U8, name=f"wg_s{b}", align_bytes=64) for b in range(BLOCKS)]

        def round_second_pass(b):
            nc.vector.tensor_copy(
                out=wg_b[:, b, 1, :, :].rearrange("p (c i) j -> p c j i", i=4),
                in_=wg_second[b][:].rearrange("p j (c i) -> p c j i", i=4),
            )

        def quantise_wg(b):
            nc.vector.quantize_mx(
                out=wg_q[b][:].bitcast(FP8X4), scales=wg_s[b][:], in_=wg_b[:, b].rearrange("p s n j -> p (s n j)")
            )

        def output_gate(b, parts, bank, o):
            width = sum(words[0].shape[1] for words, scales in parts)
            sums = psum.tile([P, width], F32, name="gate_sums", tag=bank)
            first = 0
            for words, scales in parts:
                cols = slice(first, first + words[0].shape[1])
                first = cols.stop
                for s in range(PASSES):
                    nc.tensor.matmul_mx(
                        out=sums[:, cols],
                        lhsT=wg_q[b][:, P * s : P * (s + 1)].bitcast(FP8X4),
                        lhsT_scale=wg_s[b][:, P * s : P * (s + 1)],
                        rhs=words[s].bitcast(FP8X4),
                        rhs_scale=scales[s],
                        start=(s == 0),
                        stop=(s == PASSES - 1),
                    )
            nc.scalar.activation(out=o[:], in_=sums[:], func=ACT.Sigmoid)
            return o

        for s in range(PASSES):
            gather_words(early_words[s][:], s, 0, 2)
        for first, count in ((0, 2), (2, 2)):
            for s in range(PASSES):
                gather_scales(s, first, count)
        nc.scalar.copy(
            out=wg_b[:, :, 0, :, :].rearrange("p b (c i) j -> p b c j i", i=4),
            in_=wg_first[:].rearrange("p j (b c i) -> p b c j i", b=BLOCKS, i=4),
        )
        rows0 = first_layer(0)
        late_words = [reused(f"late_words{s}", [P, PAIR], I32, 2 * s) for s in range(PASSES)]
        for e in (2, 3):
            for s in range(PASSES):
                gather_words(late_words[s][:, slots(e - 2)], s, e, 1)
                gw[s, e] = late_words[s][:, slots(e - 2)]
        round_second_pass(1)
        quantise_wg(1)
        rows1 = first_layer(1)
        cols0 = keep.tile([P, H], BF16, name="cols0", align_bytes=64)
        turn_hidden(cols0[:], rows0, "bank2", nc.vector.tensor_copy)
        codes0 = quantise_hidden(0, 1, cols0)
        cols1 = keep.tile([P, H], BF16, name="cols1", align_bytes=64)
        turn_hidden(cols1[:], rows1, "bank3", nc.vector.tensor_copy)
        codes1 = quantise_hidden(1, 1, cols1)
        y = [keep.tile([P, BLOCKS, C], F32, name=f"y{e}") for e in range(2)]
        times_weight(y[0][:], second_layer(0, 1, codes0, "bank6")[:], 0, 1)
        rows2 = first_layer(2)
        early_part = ([early_words[s][:] for s in range(PASSES)], [gs[s, 0][:] for s in range(PASSES)])
        o_first = output_gate(1, [early_part], "bank2", keep.tile([P, PAIR], F32, name="o_first"))
        rows3 = first_layer(3)
        result[1] = keep.tile([P, T], F32, name="result1")
        scatter_gated(y[0], 0, 1, o_first[:, slots(0)])
        times_weight(y[1][:], second_layer(1, 1, codes1, "bank7")[:], 1, 1)
        cols23 = keep.tile([P, 2 * H], BF16, name="cols23", align_bytes=64)
        turn_hidden(cols23[:, :H], rows2, "bank0", nc.scalar.copy)
        turn_hidden(cols23[:, H:], rows3, "bank1", nc.scalar.copy)
        codes23 = quantise_hidden(2, 2, cols23)
        round_second_pass(0)
        wg_q[0] = keep.tile([P, PASSES * P], U32, name="wg_q0", align_bytes=64)
        quantise_wg(0)
        result[0] = reused("result0", [P, T], F32, 36)
        scatter_plain(y[0], 0, 1)
        late_parts = [([w[:] for w in late_words], [gs[s, 1][:] for s in range(PASSES)])]
        o_second = output_gate(1, late_parts, "bank6", reused("o_second", [P, PAIR], F32, 40))
        scatter_gated(y[1], 1, 1, o_first[:, slots(1)])
        scatter_plain(y[1], 1, 1)
        y23 = keep.tile([P, BLOCKS, PAIR], F32, name="y23")
        times_weight(y23[:], second_layer(2, 2, codes23, "bank2")[:], 2, 2)
        tokens = ([xw[s][:] for s in range(PASSES)], [xs[:, s, :] for s in range(PASSES)])
        o_tokens = output_gate(0, [tokens], "bank0", keep.tile([P, T], F32, name="o_tokens"))
        scatter_plain(y23, 2, 2)
        scatter_gated(y23, 2, 2, o_second[:])
        nc.sync.dma_start(out=out[P:, :], in_=result[1][:])
        gated = keep.tile([P, T], F32, name="gated")
        nc.vector.tensor_tensor(out=gated[:], in0=result[0][:], in1=o_tokens[:], op=MULT)
        nc.sync.dma_start(out=out[:P, :], in_=gated[:])
